import numpy as np
import ml_dtypes


def mxq(x, axis, fmt="e4m3"):
    dtype, down = {"e4m3": (ml_dtypes.float8_e4m3fn, 7), "e5m2": (ml_dtypes.float8_e5m2, 14)}[fmt]
    v = np.moveaxis(np.asarray(x, np.float32).astype(ml_dtypes.bfloat16).astype(np.float64), axis, -1)
    blocks = v.reshape(v.shape[:-1] + (-1, 32))
    amax = np.abs(blocks).max(-1, keepdims=True)
    byte = np.maximum(np.where(amax > 0, np.frexp(amax)[1] - 1 + 127, 0) - down, 1)
    scale = np.exp2(byte - 127.0)
    codes = (blocks / scale).astype(np.float32).astype(dtype).astype(np.float64)
    return np.moveaxis((codes * scale).reshape(v.shape), -1, axis)


WIDE = False


def mx_kscale(k):
    if not WIDE:
        return np.ones(k)
    levels = np.array([10, -10, 5, -5, 0])
    if k % 512:
        return np.exp2(np.random.permutation(np.resize(levels, k // 32))).repeat(32)
    a = np.empty((k // 512, 16))
    for p in range(k // 512):
        a[p, :8] = np.random.permutation(np.resize(levels, 8))
        for g in range(8):
            far = levels[np.abs(levels - a[p, g]) >= 10]
            a[p, g + 8] = far[np.random.randint(len(far))]
    return np.exp2(a.ravel()).repeat(32)


BF16 = ml_dtypes.bfloat16


def bf(x):
    return np.asarray(x, np.float32).astype(BF16)


def f64(x):
    return np.asarray(x).astype(np.float64)


S, K, C, A = 2048, 2048, 512, 1024


def draw0():
    s = mx_kscale(K)
    u = mx_kscale(S)
    mean = 0.5 * np.random.standard_normal(K)
    spectra = mean + np.random.standard_normal((S, K))
    return {
        "spectra": bf(spectra * s),
        "mean": bf(mean * s),
        "r": bf(np.random.standard_normal((K, C)) / np.sqrt(K) / s[:, None]),
        "weight": bf(np.random.uniform(0.5, 1.5, S) * u),
        "y": bf(np.random.standard_normal((S, A)) / np.sqrt(S) / u[:, None]),
        "inv_score": bf(np.random.uniform(0.5, 1.5, C)),
    }


def core(spectra, mean, r, weight, y, inv_score):
    xc = f64(spectra) - f64(mean)
    t = mxq(xc, 1, "e4m3") @ mxq(f64(r), 0, "e4m3")
    z = t * f64(weight)[:, None]
    cov = mxq(z, 0, "e4m3").T @ mxq(f64(y), 0, "e4m3")
    return cov * f64(inv_score)[:, None]


def e4m3fn_bytes(y):
    return np.clip(np.asarray(y, np.float64), -448.0, 448.0).astype(np.float32).astype(ml_dtypes.float8_e4m3fn).view(np.uint8)


def e4m3fn_values(b):
    return np.asarray(b, np.uint8).view(ml_dtypes.float8_e4m3fn).astype(np.float64)


def setup_inputs():
    d = draw0()
    x0 = np.asarray(d['y']).astype(np.float64)
    s = (np.max(np.abs(x0), axis=(1,), keepdims=True) / 448.0).astype(np.float32)
    out = {}
    for k, v in d.items():
        if k == 'y':
            out['y_bytes'] = e4m3fn_bytes(x0 / s.astype(np.float64))
            out['y_scale'] = s
        else:
            out[k] = v
    return out


def reference(spectra, mean, r, weight, y_bytes, y_scale, inv_score):
    return core(spectra, mean, r, weight, e4m3fn_values(y_bytes) * y_scale.astype(np.float64), inv_score)

@@ -1,0 +1,344 @@
+from contextlib import ExitStack
+
+import concourse.mybir as mybir
+from concourse.masks import make_identity
+
+S, K, C, A = 2048, 2048, 512, 1024
+P = 128
+PACK = 4
+PASS = P * PACK
+G_K = K // PASS
+G_S = S // PASS
+N_TILES = S // P
+HALF_A = A // 2
+
+FLOPS = 2 * S * K * C + 2 * S * C * A
+
+F32 = mybir.dt.float32
+BF16 = mybir.dt.bfloat16
+U32 = mybir.dt.uint32
+U8 = mybir.dt.uint8
+FP8 = mybir.dt.float8_e4m3fn
+FP8X4 = mybir.dt.float8_e4m3fn_x4
+COPY = mybir.ActivationFunctionType.Copy
+MULT = mybir.AluOpType.mult
+SUB = mybir.AluOpType.subtract
+
+Y_SCALAR_COLS = 128
+
+
+def tile_pls_concentration_loadings_s7_kernel(
+    tc, spectra, mean, r, weight, y_bytes, y_scale, inv_score, out
+):
+    nc = tc.nc
+    with ExitStack() as ctx:
+        keep = ctx.enter_context(tc.tile_pool(name="keep", bufs=1))
+        work = ctx.enter_context(tc.tile_pool(name="work", bufs=3))
+        psum = ctx.enter_context(tc.psum_pool(name="psum", bufs=1))
+
+        ident = keep.tile([P, P], F32, name="ident")
+        make_identity(nc, ident[:])
+
+        ctx.enter_context(tc.manual_schedule())
+
+        mean_sb = keep.tile([P, G_K, 2, 2], BF16, name="mean_sb")
+        weight_bf = keep.tile([P, G_S, PACK], BF16, name="weight_bf")
+        weight_sb = keep.tile([P, G_S * PACK], F32, name="weight_sb")
+        y_scale_sb = keep.tile([P, G_S, PACK], F32, name="y_scale_sb")
+        inv_bf = keep.tile([P, 4, 2], BF16, name="inv_bf")
+        inv_sb = keep.tile([P, 4], F32, name="inv_sb")
+        warm = keep.tile([P, 1], F32, name="warm")
+
+        x_raw = [keep.tile([P, K], BF16, name=f"x_raw{i}", align_bytes=64) for i in range(N_TILES)]
+        r_raw = [keep.tile([P, PACK, C], BF16, name=f"r_raw{g}", align_bytes=64) for g in range(G_K)]
+        y_raw = [keep.tile([P, PACK, A], U8, name=f"y_raw{g}", align_bytes=64) for g in range(G_S)]
+
+        x_hbm = spectra.rearrange("(g p j) k -> g j p k", p=P, j=PACK)
+        r_hbm = r.rearrange("(g p j) c -> g p j c", p=P, j=PACK)
+        y_hbm = y_bytes.rearrange("(g p j) a -> g p j a", p=P, j=PACK)
+
+        def load_x(i):
+            nc.sync.dma_start(out=x_raw[i][:], in_=x_hbm[i // PACK, i % PACK])
+
+        def load_r(g):
+            nc.sync.dma_start(out=r_raw[g][:], in_=r_hbm[g])
+
+        def load_y(g):
+            nc.sync.dma_start(out=y_raw[g][:], in_=y_hbm[g])
+
+        nc.scalar.dma_start(
+            out=mean_sb[:].rearrange("p g u e -> p g (u e)"),
+            in_=mean.rearrange("(g p t) -> p g t", p=P, t=PACK),
+        )
+        nc.scalar.dma_start(
+            out=y_scale_sb[:], in_=y_scale.rearrange("(g p j) o -> p g (j o)", p=P, j=PACK)
+        )
+        nc.scalar.dma_start(
+            out=weight_bf[:], in_=weight.rearrange("(g p j) -> p g j", p=P, j=PACK)
+        )
+        nc.scalar.dma_start(
+            out=inv_bf[:, :, 0:1], in_=inv_score.rearrange("(m p o) -> p m o", p=P, o=1)
+        )
+        load_x(0)
+        for g in range(G_K):
+            load_r(g)
+        load_x(1)
+        load_y(0)
+        load_x(2)
+        load_x(3)
+        load_y(1)
+        for i in range(4, 8):
+            load_x(i)
+        load_y(2)
+        for i in range(8, 10):
+            load_x(i)
+        load_y(3)
+        for i in range(10, N_TILES):
+            load_x(i)
+
+        nc.vector.memset(warm[:], 0.0)
+        nc.scalar.activation(warm[:], warm[:], COPY)
+
+        r_codes = keep.tile([P, G_K, C], U32, name="r_codes", align_bytes=64)
+        r_scales = keep.tile([P, G_K, C], U8, name="r_scales", align_bytes=64)
+        y_codes = [keep.tile([P, A], U32, name=f"y_codes{g}", align_bytes=64) for g in range(G_S)]
+        y_scales = [keep.tile([P, A], U8, name=f"y_scales{g}", align_bytes=64) for g in range(G_S)]
+        z_codes = [keep.tile([P, C], U32, name=f"z_codes{g}", align_bytes=64) for g in range(G_S)]
+        z_scales = [keep.tile([P, C], U8, name=f"z_scales{g}", align_bytes=64) for g in range(G_S)]
+
+        def bank(b, name):
+            return psum.tile([P, 512], F32, tag=f"bank{b}", name=name)
+
+        r_grouped = {}
+
+        def interleave_r(g, engine):
+            t = work.tile([P, C, PACK], BF16, tag="r_grouped", name="r_grouped", bufs=4, align_bytes=64)
+            src = r_raw[g][:].rearrange("p j c -> p c j")
+            if engine is nc.scalar:
+                nc.scalar.copy(out=t[:], in_=src)
+            else:
+                nc.vector.tensor_copy(out=t[:], in_=src)
+            r_grouped[g] = t
+
+        def quantise_r(g):
+            nc.vector.quantize_mx(
+                out=r_codes[:, g, :].bitcast(FP8X4),
+                scales=r_scales[:, g, :],
+                in_=r_grouped[g][:].rearrange("p c j -> p (c j)"),
+            )
+
+        x_banks = {}
+        x_grouped = {}
+        x_codes = {}
+        x_scales = {}
+
+        def transpose_x(i):
+            words = x_raw[i][:].bitcast(F32)
+            for b in range(2):
+                ps = bank(b, "x_turned")
+                view = ps[:].rearrange("p (u g s) -> p u g s", u=2, g=2)
+                for gl in range(2):
+                    g = 2 * b + gl
+                    for u in range(2):
+                        nc.tensor.transpose(
+                            view[:, u, gl, :], words[:, 256 * g + u : 256 * (g + 1) : 2], ident[:]
+                        )
+                x_banks[i, b] = ps
+
+        def centre_x(i, b):
+            if b == 0:
+                x_grouped[i] = work.tile(
+                    [P, G_K, P, 2, 2], BF16, tag="x_grouped", name="x_grouped", align_bytes=64
+                )
+            nc.vector.tensor_tensor(
+                out=x_grouped[i][:, 2 * b : 2 * b + 2],
+                in0=x_banks[i, b][:].bitcast(BF16).rearrange(
+                    "p (u g s e) -> p g s u e", u=2, g=2, e=2
+                ),
+                in1=mean_sb[:, 2 * b : 2 * b + 2].unsqueeze(2).to_broadcast([P, 2, P, 2, 2]),
+                op=SUB,
+            )
+
+        def quantise_x(i, b):
+            if b == 0:
+                x_codes[i] = work.tile([P, G_K * P], U32, tag="x_codes", name="x_codes", align_bytes=64)
+                x_scales[i] = work.tile([P, G_K * P], U8, tag="x_scales", name="x_scales", align_bytes=64)
+            cols = slice(256 * b, 256 * (b + 1))
+            flat = x_grouped[i][:].rearrange("p g s u e -> p (g s u e)")
+            nc.vector.quantize_mx(
+                out=x_codes[i][:, cols].bitcast(FP8X4),
+                scales=x_scales[i][:, cols],
+                in_=flat[:, 1024 * b : 1024 * (b + 1)],
+            )
+
+        t_banks = {}
+        z_planes = {}
+        z_grouped = {}
+
+        def multiply_t(i):
+            ps = bank(2 + i % 2, "t_sum")
+            for g in range(G_K):
+                cols = slice(P * g, P * (g + 1))
+                nc.tensor.matmul_mx(
+                    out=ps[:],
+                    lhsT=x_codes[i][:, cols].bitcast(FP8X4),
+                    lhsT_scale=x_scales[i][:, cols],
+                    rhs=r_codes[:, g, :].bitcast(FP8X4),
+                    rhs_scale=r_scales[:, g, :],
+                    start=(g == 0),
+                    stop=(g == G_K - 1),
+                )
+            t_banks[i] = ps
+
+        def weigh_t(i):
+            g, j = i // PACK, i % PACK
+            if j == 0:
+                z_planes[g] = work.tile([P, PACK, C], BF16, tag="z_planes", name="z_planes", bufs=2, align_bytes=64)
+            nc.scalar.activation(
+                z_planes[g][:, j, :], t_banks[i][:], COPY, scale=weight_sb[:, i : i + 1]
+            )
+
+        def interleave_z(g, c0, c1, engine):
+            if g not in z_grouped:
+                z_grouped[g] = work.tile(
+                    [P, C, PACK], BF16, tag="z_grouped", name="z_grouped", bufs=2, align_bytes=64
+                )
+            dst = z_grouped[g][:, c0:c1, :]
+            src = z_planes[g][:, :, c0:c1].rearrange("p j c -> p c j")
+            if engine is nc.scalar:
+                nc.scalar.copy(out=dst, in_=src)
+            else:
+                nc.vector.tensor_copy(out=dst, in_=src)
+
+        def quantise_z(g, c0, c1):
+            nc.vector.quantize_mx(
+                out=z_codes[g][:, c0:c1].bitcast(FP8X4),
+                scales=z_scales[g][:, c0:c1],
+                in_=z_grouped[g][:].rearrange("p c j -> p (c j)")[:, PACK * c0 : PACK * c1],
+            )
+
+        y_planes = {}
+        y_grouped = {}
+
+        def widen_y(g, h):
+            y_planes[g, h] = work.tile(
+                [P, PACK, HALF_A], BF16, tag="y_planes", name="y_planes", align_bytes=64
+            )
+            for j in range(PACK):
+                nc.scalar.activation(
+                    y_planes[g, h][:, j, :],
+                    y_raw[g][:, j, HALF_A * h : HALF_A * (h + 1)].bitcast(FP8),
+                    COPY,
+                    scale=y_scale_sb[:, g, j : j + 1],
+                )
+
+        def interleave_y(g, h):
+            y_grouped[g, h] = work.tile(
+                [P, HALF_A, PACK], BF16, tag="y_grouped", name="y_grouped", align_bytes=64
+            )
+            cut = HALF_A - Y_SCALAR_COLS
+            dst = y_grouped[g, h][:]
+            src = y_planes[g, h][:].rearrange("p j a -> p a j")
+            nc.vector.tensor_copy(out=dst[:, :cut, :], in_=src[:, :cut, :])
+            nc.scalar.copy(out=dst[:, cut:, :], in_=src[:, cut:, :])
+
+        def quantise_y(g, h):
+            cols = slice(HALF_A * h, HALF_A * (h + 1))
+            nc.vector.quantize_mx(
+                out=y_codes[g][:, cols].bitcast(FP8X4),
+                scales=y_scales[g][:, cols],
+                in_=y_grouped[g, h][:].rearrange("p a j -> p (a j)"),
+            )
+
+        cov_banks = {}
+
+        def multiply_cov(m, h, g):
+            if g == 0:
+                b = 4 + m if h == 0 else m
+                cov_banks[m, h] = bank(b, "cov_sum")
+            c_cols = slice(P * m, P * (m + 1))
+            a_cols = slice(HALF_A * h, HALF_A * (h + 1))
+            nc.tensor.matmul_mx(
+                out=cov_banks[m, h][:],
+                lhsT=z_codes[g][:, c_cols].bitcast(FP8X4),
+                lhsT_scale=z_scales[g][:, c_cols],
+                rhs=y_codes[g][:, a_cols].bitcast(FP8X4),
+                rhs_scale=y_scales[g][:, a_cols],
+                start=(g == 0),
+                stop=(g == G_S - 1),
+            )
+
+        def store_cov(m, h):
+            res = keep.tile([P, HALF_A], F32, name=f"res{m}{h}")
+            if h == 0:
+                nc.vector.tensor_scalar(
+                    out=res[:], in0=cov_banks[m, h][:], scalar1=inv_sb[:, m : m + 1],
+                    scalar2=None, op0=MULT,
+                )
+            else:
+                nc.scalar.activation(res[:], cov_banks[m, h][:], COPY, scale=inv_sb[:, m : m + 1])
+            nc.sync.dma_start(
+                out=out[P * m : P * (m + 1), HALF_A * h : HALF_A * (h + 1)], in_=res[:]
+            )
+
+        chunks = [(g, h) for g in range(G_S) for h in range(2)]
+        widen_step = [0, 2, 3, 5, 6, 8, 10, 11]
+
+        interleave_r(1, nc.scalar)
+        interleave_r(3, nc.scalar)
+        transpose_x(0)
+        centre_x(0, 0)
+        centre_x(0, 1)
+        interleave_r(0, nc.vector)
+        quantise_x(0, 0)
+        quantise_x(0, 1)
+        quantise_r(0)
+        interleave_r(2, nc.vector)
+        quantise_r(1)
+        nc.vector.tensor_copy(out=weight_sb[:], in_=weight_bf[:].rearrange("p g j -> p (g j)"))
+        nc.vector.tensor_copy(out=inv_sb[:], in_=inv_bf[:, :, 0])
+        quantise_r(2)
+        quantise_r(3)
+        widen_y(*chunks[0])
+
+        for i in range(1, N_TILES):
+            transpose_x(i)
+            centre_x(i, 0)
+            centre_x(i, 1)
+            multiply_t(i - 1)
+            quantise_x(i, 0)
+            for n, chunk in enumerate(chunks):
+                if widen_step[n] == i:
+                    widen_y(*chunk)
+                if widen_step[n] + 1 == i:
+                    interleave_y(*chunk)
+                if widen_step[n] + 2 == i:
+                    quantise_y(*chunk)
+            if i % PACK == 1 and i > 1:
+                interleave_z(i // PACK - 1, 0, C, nc.vector)
+            quantise_x(i, 1)
+            weigh_t(i - 1)
+            if i % PACK == 2 and i > 2:
+                quantise_z(i // PACK - 1, 0, C)
+            if i % PACK == 3 and i > 3:
+                for m in range(4):
+                    multiply_cov(m, 0, i // PACK - 1)
+
+        for g in range(G_S - 1):
+            multiply_cov(0, 1, g)
+        multiply_t(N_TILES - 1)
+        weigh_t(N_TILES - 1)
+        for m in range(1, 4):
+            for g in range(G_S - 1):
+                multiply_cov(m, 1, g)
+
+        last = G_S - 1
+        interleave_z(last, 384, C, nc.scalar)
+        interleave_z(last, 0, 256, nc.vector)
+        interleave_z(last, 256, 384, nc.vector)
+        quantise_z(last, 0, 256)
+        quantise_z(last, 256, C)
+        for m in range(4):
+            for h in range(2):
+                multiply_cov(m, h, last)
+                store_cov(m, h)

@@ -23,8 +23,7 @@ FP8X4 = mybir.dt.float8_e4m3fn_x4
 COPY = mybir.ActivationFunctionType.Copy
 MULT = mybir.AluOpType.mult
 SUB = mybir.AluOpType.subtract
-
-Y_SCALAR_COLS = 128
+ADD = mybir.AluOpType.add
 
 
 def tile_pls_concentration_loadings_s7_kernel(
@@ -57,8 +56,10 @@ def tile_pls_concentration_loadings_s7_kernel(
         r_hbm = r.rearrange("(g p j) c -> g p j c", p=P, j=PACK)
         y_hbm = y_bytes.rearrange("(g p j) a -> g p j a", p=P, j=PACK)
 
-        def load_x(i):
-            nc.sync.dma_start(out=x_raw[i][:], in_=x_hbm[i // PACK, i % PACK])
+        def load_x(i, pieces=1):
+            for n in range(pieces):
+                cols = slice(K * n // pieces, K * (n + 1) // pieces)
+                nc.sync.dma_start(out=x_raw[i][:, cols], in_=x_hbm[i // PACK, i % PACK][:, cols])
 
         def load_r(g):
             nc.sync.dma_start(out=r_raw[g][:], in_=r_hbm[g])
@@ -79,7 +80,7 @@ def tile_pls_concentration_loadings_s7_kernel(
         nc.scalar.dma_start(
             out=inv_bf[:, :, 0:1], in_=inv_score.rearrange("(m p o) -> p m o", p=P, o=1)
         )
-        load_x(0)
+        load_x(0, 2)
         for g in range(G_K):
             load_r(g)
         load_x(1)
@@ -175,27 +176,27 @@ def tile_pls_concentration_loadings_s7_kernel(
         z_planes = {}
         z_grouped = {}
 
-        def multiply_t(i):
-            ps = bank(2 + i % 2, "t_sum")
+        def multiply_t(i, b, c0, c1):
+            ps = bank(b, "t_sum")
             for g in range(G_K):
                 cols = slice(P * g, P * (g + 1))
                 nc.tensor.matmul_mx(
-                    out=ps[:],
+                    out=ps[:, : c1 - c0],
                     lhsT=x_codes[i][:, cols].bitcast(FP8X4),
                     lhsT_scale=x_scales[i][:, cols],
-                    rhs=r_codes[:, g, :].bitcast(FP8X4),
-                    rhs_scale=r_scales[:, g, :],
+                    rhs=r_codes[:, g, c0:c1].bitcast(FP8X4),
+                    rhs_scale=r_scales[:, g, c0:c1],
                     start=(g == 0),
                     stop=(g == G_K - 1),
                 )
-            t_banks[i] = ps
+            t_banks[i, c0] = ps
 
-        def weigh_t(i):
+        def weigh_t(i, c0, c1):
             g, j = i // PACK, i % PACK
-            if j == 0:
+            if g not in z_planes:
                 z_planes[g] = work.tile([P, PACK, C], BF16, tag="z_planes", name="z_planes", bufs=2, align_bytes=64)
             nc.scalar.activation(
-                z_planes[g][:, j, :], t_banks[i][:], COPY, scale=weight_sb[:, i : i + 1]
+                z_planes[g][:, j, c0:c1], t_banks[i, c0][:, : c1 - c0], COPY, scale=weight_sb[:, i : i + 1]
             )
 
         def interleave_z(g, c0, c1, engine):
@@ -219,6 +220,7 @@ def tile_pls_concentration_loadings_s7_kernel(
 
         y_planes = {}
         y_grouped = {}
+        y_pooled = {}
 
         def widen_y(g, h):
             y_planes[g, h] = work.tile(
@@ -232,22 +234,33 @@ def tile_pls_concentration_loadings_s7_kernel(
                     scale=y_scale_sb[:, g, j : j + 1],
                 )
 
-        def interleave_y(g, h):
-            y_grouped[g, h] = work.tile(
-                [P, HALF_A, PACK], BF16, tag="y_grouped", name="y_grouped", align_bytes=64
-            )
-            cut = HALF_A - Y_SCALAR_COLS
-            dst = y_grouped[g, h][:]
-            src = y_planes[g, h][:].rearrange("p j a -> p a j")
-            nc.vector.tensor_copy(out=dst[:, :cut, :], in_=src[:, :cut, :])
-            nc.scalar.copy(out=dst[:, cut:, :], in_=src[:, cut:, :])
+        def interleave_y(g, h, a0, a1, engine):
+            if engine is nc.gpsimd:
+                t = work.tile([P, a1 - a0, PACK], BF16, tag="y_pooled", name="y_pooled", bufs=1, align_bytes=64)
+            elif (g, h) not in y_grouped:
+                t = work.tile([P, HALF_A, PACK], BF16, tag="y_grouped", name="y_grouped", align_bytes=64)
+                y_grouped[g, h] = t
+            else:
+                t = y_grouped[g, h]
+            src = y_planes[g, h][:, :, a0:a1].rearrange("p j a -> p a j")
+            if engine is nc.gpsimd:
+                nc.gpsimd.tensor_scalar(out=t[:], in0=src, scalar1=1.0, scalar2=0.0, op0=MULT, op1=ADD)
+                y_pooled[g, h, a0] = t
+            elif engine is nc.scalar:
+                nc.scalar.copy(out=t[:, a0:a1, :], in_=src)
+            else:
+                nc.vector.tensor_copy(out=t[:, a0:a1, :], in_=src)
 
-        def quantise_y(g, h):
-            cols = slice(HALF_A * h, HALF_A * (h + 1))
+        def quantise_y(g, h, a0, a1, pooled=False):
+            cols = slice(HALF_A * h + a0, HALF_A * h + a1)
+            if pooled:
+                src = y_pooled[g, h, a0][:]
+            else:
+                src = y_grouped[g, h][:, a0:a1, :]
             nc.vector.quantize_mx(
                 out=y_codes[g][:, cols].bitcast(FP8X4),
                 scales=y_scales[g][:, cols],
-                in_=y_grouped[g, h][:].rearrange("p a j -> p (a j)"),
+                in_=src.rearrange("p a j -> p (a j)"),
             )
 
         cov_banks = {}
@@ -268,9 +281,9 @@ def tile_pls_concentration_loadings_s7_kernel(
                 stop=(g == G_S - 1),
             )
 
-        def store_cov(m, h):
+        def store_cov(m, h, engine):
             res = keep.tile([P, HALF_A], F32, name=f"res{m}{h}")
-            if h == 0:
+            if engine is nc.vector:
                 nc.vector.tensor_scalar(
                     out=res[:], in0=cov_banks[m, h][:], scalar1=inv_sb[:, m : m + 1],
                     scalar2=None, op0=MULT,
@@ -281,64 +294,81 @@ def tile_pls_concentration_loadings_s7_kernel(
                 out=out[P * m : P * (m + 1), HALF_A * h : HALF_A * (h + 1)], in_=res[:]
             )
 
-        chunks = [(g, h) for g in range(G_S) for h in range(2)]
-        widen_step = [0, 2, 3, 5, 6, 8, 10, 11]
+        chunks = [(0, 0), (1, 0), (0, 1), (2, 0), (1, 1), (3, 0), (2, 1), (3, 1)]
+        last = G_S - 1
 
-        interleave_r(1, nc.scalar)
-        interleave_r(3, nc.scalar)
         transpose_x(0)
-        centre_x(0, 0)
-        centre_x(0, 1)
-        interleave_r(0, nc.vector)
-        quantise_x(0, 0)
-        quantise_x(0, 1)
-        quantise_r(0)
-        interleave_r(2, nc.vector)
-        quantise_r(1)
-        nc.vector.tensor_copy(out=weight_sb[:], in_=weight_bf[:].rearrange("p g j -> p (g j)"))
-        nc.vector.tensor_copy(out=inv_sb[:], in_=inv_bf[:, :, 0])
-        quantise_r(2)
-        quantise_r(3)
-        widen_y(*chunks[0])
-
-        for i in range(1, N_TILES):
-            transpose_x(i)
+        interleave_r(0, nc.scalar)
+        interleave_r(2, nc.scalar)
+        for i in range(N_TILES):
+            n, piece = (i - 1) // 2, (i - 1) % 2
+            if i > 0:
+                interleave_y(*chunks[n], 128 * piece, 128 * (piece + 1), nc.gpsimd)
             centre_x(i, 0)
             centre_x(i, 1)
-            multiply_t(i - 1)
+            if i > 0 and i % 2 == 0:
+                quantise_y(*chunks[n], 256, HALF_A)
             quantise_x(i, 0)
-            for n, chunk in enumerate(chunks):
-                if widen_step[n] == i:
-                    widen_y(*chunk)
-                if widen_step[n] + 1 == i:
-                    interleave_y(*chunk)
-                if widen_step[n] + 2 == i:
-                    quantise_y(*chunk)
-            if i % PACK == 1 and i > 1:
-                interleave_z(i // PACK - 1, 0, C, nc.vector)
             quantise_x(i, 1)
-            weigh_t(i - 1)
+            if i + 1 < N_TILES:
+                transpose_x(i + 1)
+            if i == 0:
+                interleave_r(1, nc.vector)
+                quantise_r(0)
+                quantise_r(1)
+                interleave_r(3, nc.vector)
+                nc.vector.tensor_copy(
+                    out=weight_sb[:], in_=weight_bf[:].rearrange("p g j -> p (g j)")
+                )
+                nc.vector.tensor_copy(out=inv_sb[:], in_=inv_bf[:, :, 0])
+                quantise_r(2)
+                quantise_r(3)
+            if i + 1 < N_TILES:
+                multiply_t(i, 2 + i % 2, 0, C)
+            else:
+                for m in range(4):
+                    multiply_cov(m, 0, 2)
+                multiply_t(i, 3, 0, 256)
+                multiply_t(i, 1, 256, C)
+            if i % PACK == 1 and i > 1:
+                interleave_z(i // PACK - 1, 384, C, nc.scalar)
+                interleave_z(i // PACK - 1, 0, 384, nc.vector)
             if i % PACK == 2 and i > 2:
                 quantise_z(i // PACK - 1, 0, C)
-            if i % PACK == 3 and i > 3:
-                for m in range(4):
-                    multiply_cov(m, 0, i // PACK - 1)
+            if i + 1 == N_TILES:
+                weigh_t(i - 1, 0, C)
+                weigh_t(i, 0, 256)
+                weigh_t(i, 256, C)
+                interleave_y(*chunks[n], 320, HALF_A, nc.scalar)
+                interleave_y(*chunks[n], 128, 320, nc.vector)
+            elif i % 2 == 1:
+                interleave_y(*chunks[n], 256, HALF_A, nc.scalar)
 
-        for g in range(G_S - 1):
-            multiply_cov(0, 1, g)
-        multiply_t(N_TILES - 1)
-        weigh_t(N_TILES - 1)
-        for m in range(1, 4):
+            if i > 0:
+                quantise_y(*chunks[n], 128 * piece, 128 * (piece + 1), pooled=True)
+            if i % 2 == 0:
+                widen_y(*chunks[i // 2])
+            if 0 < i < N_TILES - 1:
+                weigh_t(i - 1, 0, C)
+            if i in (7, 8, 9, 10, 11, 12, 13, 14):
+                multiply_cov((i - 7) % PACK, 0, (i - 7) // PACK)
+
+        for m in (0, 2):
             for g in range(G_S - 1):
                 multiply_cov(m, 1, g)
-
-        last = G_S - 1
         interleave_z(last, 384, C, nc.scalar)
         interleave_z(last, 0, 256, nc.vector)
+        quantise_y(3, 1, 128, 256)
         interleave_z(last, 256, 384, nc.vector)
         quantise_z(last, 0, 256)
         quantise_z(last, 256, C)
+        quantise_y(3, 1, 256, HALF_A)
         for m in range(4):
-            for h in range(2):
-                multiply_cov(m, h, last)
-                store_cov(m, h)
+            multiply_cov(m, 0, last)
+            store_cov(m, 0, nc.vector if m % 2 else nc.scalar)
+        for m in (3, 1):
+            for g in range(G_S - 1):
+                multiply_cov(m, 1, g)
+        for m in (0, 2, 3, 1):
+            multiply_cov(m, 1, last)
+            store_cov(m, 1, nc.vector if m in (2, 1) else nc.scalar)

@@ -47,6 +47,7 @@ def tile_pls_concentration_loadings_s7_kernel(
         inv_bf = keep.tile([P, 4, 2], BF16, name="inv_bf")
         inv_sb = keep.tile([P, 4], F32, name="inv_sb")
         warm = keep.tile([P, 1], F32, name="warm")
+        zeros = keep.tile([P, 512], BF16, name="zeros")
 
         x_raw = [keep.tile([P, K], BF16, name=f"x_raw{i}", align_bytes=64) for i in range(N_TILES)]
         r_raw = [keep.tile([P, PACK, C], BF16, name=f"r_raw{g}", align_bytes=64) for g in range(G_K)]
@@ -67,24 +68,25 @@ def tile_pls_concentration_loadings_s7_kernel(
         def load_y(g):
             nc.sync.dma_start(out=y_raw[g][:], in_=y_hbm[g])
 
+        nc.vector.memset(zeros[:], 0.0)
         nc.scalar.dma_start(
             out=mean_sb[:].rearrange("p g u e -> p g (u e)"),
             in_=mean.rearrange("(g p t) -> p g t", p=P, t=PACK),
-        )
-        nc.scalar.dma_start(
-            out=y_scale_sb[:], in_=y_scale.rearrange("(g p j) o -> p g (j o)", p=P, j=PACK)
-        )
-        nc.scalar.dma_start(
-            out=weight_bf[:], in_=weight.rearrange("(g p j) -> p g j", p=P, j=PACK)
-        )
-        nc.scalar.dma_start(
-            out=inv_bf[:, :, 0:1], in_=inv_score.rearrange("(m p o) -> p m o", p=P, o=1)
         )
         load_x(0, 2)
         for g in range(G_K):
             load_r(g)
         load_x(1)
         load_y(0)
+        nc.sync.dma_start(
+            out=y_scale_sb[:], in_=y_scale.rearrange("(g p j) o -> p g (j o)", p=P, j=PACK)
+        )
+        nc.sync.dma_start(
+            out=weight_bf[:], in_=weight.rearrange("(g p j) -> p g j", p=P, j=PACK)
+        )
+        nc.sync.dma_start(
+            out=inv_bf[:, :, 0:1], in_=inv_score.rearrange("(m p o) -> p m o", p=P, o=1)
+        )
         load_x(2)
         load_x(3)
         load_y(1)
@@ -110,15 +112,19 @@ def tile_pls_concentration_loadings_s7_kernel(
         def bank(b, name):
             return psum.tile([P, 512], F32, tag=f"bank{b}", name=name)
 
+        def interleave(engine, dst, src):
+            dst = dst.rearrange("p (a i) j -> p a j i", i=4)
+            src = src.rearrange("p j (a i) -> p a j i", i=4)
+            if engine is nc.scalar:
+                nc.scalar.copy(out=dst, in_=src)
+            else:
+                nc.vector.tensor_copy(out=dst, in_=src)
+
         r_grouped = {}
 
         def interleave_r(g, engine):
             t = work.tile([P, C, PACK], BF16, tag="r_grouped", name="r_grouped", bufs=4, align_bytes=64)
-            src = r_raw[g][:].rearrange("p j c -> p c j")
-            if engine is nc.scalar:
-                nc.scalar.copy(out=t[:], in_=src)
-            else:
-                nc.vector.tensor_copy(out=t[:], in_=src)
+            interleave(engine, t[:], r_raw[g][:])
             r_grouped[g] = t
 
         def quantise_r(g):
@@ -204,12 +210,7 @@ def tile_pls_concentration_loadings_s7_kernel(
                 z_grouped[g] = work.tile(
                     [P, C, PACK], BF16, tag="z_grouped", name="z_grouped", bufs=2, align_bytes=64
                 )
-            dst = z_grouped[g][:, c0:c1, :]
-            src = z_planes[g][:, :, c0:c1].rearrange("p j c -> p c j")
-            if engine is nc.scalar:
-                nc.scalar.copy(out=dst, in_=src)
-            else:
-                nc.vector.tensor_copy(out=dst, in_=src)
+            interleave(engine, z_grouped[g][:, c0:c1, :], z_planes[g][:, :, c0:c1])
 
         def quantise_z(g, c0, c1):
             nc.vector.quantize_mx(
@@ -242,14 +243,15 @@ def tile_pls_concentration_loadings_s7_kernel(
                 y_grouped[g, h] = t
             else:
                 t = y_grouped[g, h]
-            src = y_planes[g, h][:, :, a0:a1].rearrange("p j a -> p a j")
+            src = y_planes[g, h][:, :, a0:a1]
             if engine is nc.gpsimd:
-                nc.gpsimd.tensor_scalar(out=t[:], in0=src, scalar1=1.0, scalar2=0.0, op0=MULT, op1=ADD)
+                nc.gpsimd.tensor_scalar(
+                    out=t[:], in0=src.rearrange("p j a -> p a j"),
+                    scalar1=1.0, scalar2=0.0, op0=MULT, op1=ADD,
+                )
                 y_pooled[g, h, a0] = t
-            elif engine is nc.scalar:
-                nc.scalar.copy(out=t[:, a0:a1, :], in_=src)
             else:
-                nc.vector.tensor_copy(out=t[:, a0:a1, :], in_=src)
+                interleave(engine, t[:, a0:a1, :], src)
 
         def quantise_y(g, h, a0, a1, pooled=False):
             cols = slice(HALF_A * h + a0, HALF_A * h + a1)
@@ -297,6 +299,9 @@ def tile_pls_concentration_loadings_s7_kernel(
         chunks = [(0, 0), (1, 0), (0, 1), (2, 0), (1, 1), (3, 0), (2, 1), (3, 1)]
         last = G_S - 1
 
+        idle = bank(7, "idle")
+        for n in range(3):
+            nc.tensor.matmul(idle[:], lhsT=zeros[:, :P], rhs=zeros[:], start=True, stop=True)
         transpose_x(0)
         interleave_r(0, nc.scalar)
         interleave_r(2, nc.scalar)
@@ -306,10 +311,15 @@ def tile_pls_concentration_loadings_s7_kernel(
                 interleave_y(*chunks[n], 128 * piece, 128 * (piece + 1), nc.gpsimd)
             centre_x(i, 0)
             centre_x(i, 1)
-            if i > 0 and i % 2 == 0:
+            if i > 0 and i % 2 == 0 and i < 14:
                 quantise_y(*chunks[n], 256, HALF_A)
             quantise_x(i, 0)
             quantise_x(i, 1)
+            if i == 1:
+                nc.vector.tensor_copy(
+                    out=weight_sb[:], in_=weight_bf[:].rearrange("p g j -> p (g j)")
+                )
+                nc.vector.tensor_copy(out=inv_sb[:], in_=inv_bf[:, :, 0])
             if i + 1 < N_TILES:
                 transpose_x(i + 1)
             if i == 0:
@@ -317,10 +327,6 @@ def tile_pls_concentration_loadings_s7_kernel(
                 quantise_r(0)
                 quantise_r(1)
                 interleave_r(3, nc.vector)
-                nc.vector.tensor_copy(
-                    out=weight_sb[:], in_=weight_bf[:].rearrange("p g j -> p (g j)")
-                )
-                nc.vector.tensor_copy(out=inv_sb[:], in_=inv_bf[:, :, 0])
                 quantise_r(2)
                 quantise_r(3)
             if i + 1 < N_TILES:
@@ -339,8 +345,9 @@ def tile_pls_concentration_loadings_s7_kernel(
                 weigh_t(i - 1, 0, C)
                 weigh_t(i, 0, 256)
                 weigh_t(i, 256, C)
-                interleave_y(*chunks[n], 320, HALF_A, nc.scalar)
-                interleave_y(*chunks[n], 128, 320, nc.vector)
+                interleave_y(*chunks[n], 384, HALF_A, nc.scalar)
+                quantise_y(2, 1, 256, HALF_A)
+                interleave_y(*chunks[n], 128, 384, nc.vector)
             elif i % 2 == 1:
                 interleave_y(*chunks[n], 256, HALF_A, nc.scalar)
 
@@ -356,10 +363,9 @@ def tile_pls_concentration_loadings_s7_kernel(
         for m in (0, 2):
             for g in range(G_S - 1):
                 multiply_cov(m, 1, g)
-        interleave_z(last, 384, C, nc.scalar)
         interleave_z(last, 0, 256, nc.vector)
         quantise_y(3, 1, 128, 256)
-        interleave_z(last, 256, 384, nc.vector)
+        interleave_z(last, 256, C, nc.vector)
         quantise_z(last, 0, 256)
         quantise_z(last, 256, C)
         quantise_y(3, 1, 256, HALF_A)

@@ -122,10 +122,10 @@ def tile_pls_concentration_loadings_s7_kernel(
 
         r_grouped = {}
 
-        def interleave_r(g, engine):
-            t = work.tile([P, C, PACK], BF16, tag="r_grouped", name="r_grouped", bufs=4, align_bytes=64)
-            interleave(engine, t[:], r_raw[g][:])
-            r_grouped[g] = t
+        def interleave_r(g, c0, c1, engine):
+            if g not in r_grouped:
+                r_grouped[g] = work.tile([P, C, PACK], BF16, tag="r_grouped", name="r_grouped", bufs=4, align_bytes=64)
+            interleave(engine, r_grouped[g][:, c0:c1, :], r_raw[g][:, :, c0:c1])
 
         def quantise_r(g):
             nc.vector.quantize_mx(
@@ -303,16 +303,16 @@ def tile_pls_concentration_loadings_s7_kernel(
         for n in range(3):
             nc.tensor.matmul(idle[:], lhsT=zeros[:, :P], rhs=zeros[:], start=True, stop=True)
         transpose_x(0)
-        interleave_r(0, nc.scalar)
-        interleave_r(2, nc.scalar)
+        interleave_r(0, 0, C, nc.scalar)
+        interleave_r(2, 0, C, nc.scalar)
         for i in range(N_TILES):
-            n, piece = (i - 1) // 2, (i - 1) % 2
-            if i > 0:
+            n, piece = (i - 2) // 2, (i - 2) % 2
+            if i > 1:
                 interleave_y(*chunks[n], 128 * piece, 128 * (piece + 1), nc.gpsimd)
             centre_x(i, 0)
             centre_x(i, 1)
-            if i > 0 and i % 2 == 0 and i < 14:
-                quantise_y(*chunks[n], 256, HALF_A)
+            if i > 2 and i % 2 == 1 and i < 15:
+                quantise_y(*chunks[(i - 3) // 2], 256, HALF_A)
             quantise_x(i, 0)
             quantise_x(i, 1)
             if i == 1:
@@ -323,10 +323,11 @@ def tile_pls_concentration_loadings_s7_kernel(
             if i + 1 < N_TILES:
                 transpose_x(i + 1)
             if i == 0:
-                interleave_r(1, nc.vector)
+                interleave_r(1, 0, C, nc.vector)
                 quantise_r(0)
                 quantise_r(1)
-                interleave_r(3, nc.vector)
+                interleave_r(3, 384, C, nc.scalar)
+                interleave_r(3, 0, 384, nc.vector)
                 quantise_r(2)
                 quantise_r(3)
             if i + 1 < N_TILES:
@@ -341,25 +342,27 @@ def tile_pls_concentration_loadings_s7_kernel(
                 interleave_z(i // PACK - 1, 0, 384, nc.vector)
             if i % PACK == 2 and i > 2:
                 quantise_z(i // PACK - 1, 0, C)
-            if i + 1 == N_TILES:
+            if i % 2 == 1 and i < 15:
+                widen_y(*chunks[(i - 1) // 2])
+            elif i % 2 == 0 and i > 0:
+                interleave_y(*chunks[(i - 2) // 2], 256, HALF_A, nc.scalar)
+            if i == 14:
+                widen_y(*chunks[7])
+            if i > 0:
                 weigh_t(i - 1, 0, C)
+            if i + 1 == N_TILES:
                 weigh_t(i, 0, 256)
                 weigh_t(i, 256, C)
-                interleave_y(*chunks[n], 384, HALF_A, nc.scalar)
-                quantise_y(2, 1, 256, HALF_A)
-                interleave_y(*chunks[n], 128, 384, nc.vector)
-            elif i % 2 == 1:
-                interleave_y(*chunks[n], 256, HALF_A, nc.scalar)
-
-            if i > 0:
+            if i > 1:
                 quantise_y(*chunks[n], 128 * piece, 128 * (piece + 1), pooled=True)
-            if i % 2 == 0:
-                widen_y(*chunks[i // 2])
-            if 0 < i < N_TILES - 1:
-                weigh_t(i - 1, 0, C)
             if i in (7, 8, 9, 10, 11, 12, 13, 14):
                 multiply_cov((i - 7) % PACK, 0, (i - 7) // PACK)
 
+        quantise_y(2, 1, 256, HALF_A)
+        interleave_y(3, 1, 0, 128, nc.gpsimd)
+        interleave_y(3, 1, 320, HALF_A, nc.scalar)
+        interleave_y(3, 1, 128, 320, nc.vector)
+        quantise_y(3, 1, 0, 128, pooled=True)
         for m in (0, 2):
             for g in range(G_S - 1):
                 multiply_cov(m, 1, g)

from contextlib import ExitStack

import concourse.mybir as mybir
from concourse.masks import make_identity

S, K, C, A = 2048, 2048, 512, 1024
P = 128
PACK = 4
PASS = P * PACK
G_K = K // PASS
G_S = S // PASS
N_TILES = S // P
HALF_A = A // 2

FLOPS = 2 * S * K * C + 2 * S * C * A

F32 = mybir.dt.float32
BF16 = mybir.dt.bfloat16
U32 = mybir.dt.uint32
U8 = mybir.dt.uint8
FP8 = mybir.dt.float8_e4m3fn
FP8X4 = mybir.dt.float8_e4m3fn_x4
COPY = mybir.ActivationFunctionType.Copy
MULT = mybir.AluOpType.mult
SUB = mybir.AluOpType.subtract
ADD = mybir.AluOpType.add


def tile_pls_concentration_loadings_s7_kernel(
    tc, spectra, mean, r, weight, y_bytes, y_scale, inv_score, out
):
    nc = tc.nc
    with ExitStack() as ctx:
        keep = ctx.enter_context(tc.tile_pool(name="keep", bufs=1))
        work = ctx.enter_context(tc.tile_pool(name="work", bufs=3))
        psum = ctx.enter_context(tc.psum_pool(name="psum", bufs=1))

        ident = keep.tile([P, P], F32, name="ident")
        make_identity(nc, ident[:])

        ctx.enter_context(tc.manual_schedule())

        mean_sb = keep.tile([P, G_K, 2, 2], BF16, name="mean_sb")
        weight_bf = keep.tile([P, G_S, PACK], BF16, name="weight_bf")
        weight_sb = keep.tile([P, G_S * PACK], F32, name="weight_sb")
        y_scale_sb = keep.tile([P, G_S, PACK], F32, name="y_scale_sb")
        inv_bf = keep.tile([P, 4, 2], BF16, name="inv_bf")
        inv_sb = keep.tile([P, 4], F32, name="inv_sb")
        warm = keep.tile([P, 1], F32, name="warm")
        zeros = keep.tile([P, 512], BF16, name="zeros")

        x_raw = [keep.tile([P, K], BF16, name=f"x_raw{i}", align_bytes=64) for i in range(N_TILES)]
        r_raw = [keep.tile([P, PACK, C], BF16, name=f"r_raw{g}", align_bytes=64) for g in range(G_K)]
        y_raw = [keep.tile([P, PACK, A], U8, name=f"y_raw{g}", align_bytes=64) for g in range(G_S)]

        x_hbm = spectra.rearrange("(g p j) k -> g j p k", p=P, j=PACK)
        r_hbm = r.rearrange("(g p j) c -> g p j c", p=P, j=PACK)
        y_hbm = y_bytes.rearrange("(g p j) a -> g p j a", p=P, j=PACK)

        def load_x(i, pieces=1):
            for n in range(pieces):
                cols = slice(K * n // pieces, K * (n + 1) // pieces)
                nc.sync.dma_start(out=x_raw[i][:, cols], in_=x_hbm[i // PACK, i % PACK][:, cols])

        def load_r(g):
            nc.sync.dma_start(out=r_raw[g][:], in_=r_hbm[g])

        def load_y(g):
            nc.sync.dma_start(out=y_raw[g][:], in_=y_hbm[g])

        nc.vector.memset(zeros[:], 0.0)
        nc.scalar.dma_start(
            out=mean_sb[:].rearrange("p g u e -> p g (u e)"),
            in_=mean.rearrange("(g p t) -> p g t", p=P, t=PACK),
        )
        load_x(0, 2)
        for g in range(G_K):
            load_r(g)
        load_x(1)
        load_y(0)
        nc.sync.dma_start(
            out=y_scale_sb[:], in_=y_scale.rearrange("(g p j) o -> p g (j o)", p=P, j=PACK)
        )
        nc.sync.dma_start(
            out=weight_bf[:], in_=weight.rearrange("(g p j) -> p g j", p=P, j=PACK)
        )
        nc.sync.dma_start(
            out=inv_bf[:, :, 0:1], in_=inv_score.rearrange("(m p o) -> p m o", p=P, o=1)
        )
        load_x(2)
        load_x(3)
        load_y(1)
        for i in range(4, 8):
            load_x(i)
        load_y(2)
        for i in range(8, 10):
            load_x(i)
        load_y(3)
        for i in range(10, N_TILES):
            load_x(i)

        nc.vector.memset(warm[:], 0.0)
        nc.scalar.activation(warm[:], warm[:], COPY)

        r_codes = keep.tile([P, G_K, C], U32, name="r_codes", align_bytes=64)
        r_scales = keep.tile([P, G_K, C], U8, name="r_scales", align_bytes=64)
        y_codes = [keep.tile([P, A], U32, name=f"y_codes{g}", align_bytes=64) for g in range(G_S)]
        y_scales = [keep.tile([P, A], U8, name=f"y_scales{g}", align_bytes=64) for g in range(G_S)]
        z_codes = [keep.tile([P, C], U32, name=f"z_codes{g}", align_bytes=64) for g in range(G_S)]
        z_scales = [keep.tile([P, C], U8, name=f"z_scales{g}", align_bytes=64) for g in range(G_S)]

        def bank(b, name):
            return psum.tile([P, 512], F32, tag=f"bank{b}", name=name)

        def interleave(engine, dst, src):
            dst = dst.rearrange("p (a i) j -> p a j i", i=4)
            src = src.rearrange("p j (a i) -> p a j i", i=4)
            if engine is nc.scalar:
                nc.scalar.copy(out=dst, in_=src)
            else:
                nc.vector.tensor_copy(out=dst, in_=src)

        r_grouped = {}

        def interleave_r(g, c0, c1, engine):
            if g not in r_grouped:
                r_grouped[g] = work.tile([P, C, PACK], BF16, tag="r_grouped", name="r_grouped", bufs=4, align_bytes=64)
            interleave(engine, r_grouped[g][:, c0:c1, :], r_raw[g][:, :, c0:c1])

        def quantise_r(g):
            nc.vector.quantize_mx(
                out=r_codes[:, g, :].bitcast(FP8X4),
                scales=r_scales[:, g, :],
                in_=r_grouped[g][:].rearrange("p c j -> p (c j)"),
            )

        x_banks = {}
        x_grouped = {}
        x_codes = {}
        x_scales = {}

        def transpose_x(i):
            words = x_raw[i][:].bitcast(F32)
            for b in range(2):
                ps = bank(b, "x_turned")
                view = ps[:].rearrange("p (u g s) -> p u g s", u=2, g=2)
                for gl in range(2):
                    g = 2 * b + gl
                    for u in range(2):
                        nc.tensor.transpose(
                            view[:, u, gl, :], words[:, 256 * g + u : 256 * (g + 1) : 2], ident[:]
                        )
                x_banks[i, b] = ps

        def centre_x(i, b):
            if b == 0:
                x_grouped[i] = work.tile(
                    [P, G_K, P, 2, 2], BF16, tag="x_grouped", name="x_grouped", align_bytes=64
                )
            nc.vector.tensor_tensor(
                out=x_grouped[i][:, 2 * b : 2 * b + 2],
                in0=x_banks[i, b][:].bitcast(BF16).rearrange(
                    "p (u g s e) -> p g s u e", u=2, g=2, e=2
                ),
                in1=mean_sb[:, 2 * b : 2 * b + 2].unsqueeze(2).to_broadcast([P, 2, P, 2, 2]),
                op=SUB,
            )

        def quantise_x(i, b):
            if b == 0:
                x_codes[i] = work.tile([P, G_K * P], U32, tag="x_codes", name="x_codes", align_bytes=64)
                x_scales[i] = work.tile([P, G_K * P], U8, tag="x_scales", name="x_scales", align_bytes=64)
            cols = slice(256 * b, 256 * (b + 1))
            flat = x_grouped[i][:].rearrange("p g s u e -> p (g s u e)")
            nc.vector.quantize_mx(
                out=x_codes[i][:, cols].bitcast(FP8X4),
                scales=x_scales[i][:, cols],
                in_=flat[:, 1024 * b : 1024 * (b + 1)],
            )

        t_banks = {}
        z_planes = {}
        z_grouped = {}

        def multiply_t(i, b, c0, c1):
            ps = bank(b, "t_sum")
            for g in range(G_K):
                cols = slice(P * g, P * (g + 1))
                nc.tensor.matmul_mx(
                    out=ps[:, : c1 - c0],
                    lhsT=x_codes[i][:, cols].bitcast(FP8X4),
                    lhsT_scale=x_scales[i][:, cols],
                    rhs=r_codes[:, g, c0:c1].bitcast(FP8X4),
                    rhs_scale=r_scales[:, g, c0:c1],
                    start=(g == 0),
                    stop=(g == G_K - 1),
                )
            t_banks[i, c0] = ps

        def weigh_t(i, c0, c1):
            g, j = i // PACK, i % PACK
            if g not in z_planes:
                z_planes[g] = work.tile([P, PACK, C], BF16, tag="z_planes", name="z_planes", bufs=2, align_bytes=64)
            nc.scalar.activation(
                z_planes[g][:, j, c0:c1], t_banks[i, c0][:, : c1 - c0], COPY, scale=weight_sb[:, i : i + 1]
            )

        def interleave_z(g, c0, c1, engine):
            if g not in z_grouped:
                z_grouped[g] = work.tile(
                    [P, C, PACK], BF16, tag="z_grouped", name="z_grouped", bufs=2, align_bytes=64
                )
            interleave(engine, z_grouped[g][:, c0:c1, :], z_planes[g][:, :, c0:c1])

        def quantise_z(g, c0, c1):
            nc.vector.quantize_mx(
                out=z_codes[g][:, c0:c1].bitcast(FP8X4),
                scales=z_scales[g][:, c0:c1],
                in_=z_grouped[g][:].rearrange("p c j -> p (c j)")[:, PACK * c0 : PACK * c1],
            )

        y_planes = {}
        y_grouped = {}
        y_pooled = {}

        def widen_y(g, h):
            y_planes[g, h] = work.tile(
                [P, PACK, HALF_A], BF16, tag="y_planes", name="y_planes", align_bytes=64
            )
            for j in range(PACK):
                nc.scalar.activation(
                    y_planes[g, h][:, j, :],
                    y_raw[g][:, j, HALF_A * h : HALF_A * (h + 1)].bitcast(FP8),
                    COPY,
                    scale=y_scale_sb[:, g, j : j + 1],
                )

        def interleave_y(g, h, a0, a1, engine):
            if engine is nc.gpsimd:
                t = work.tile([P, a1 - a0, PACK], BF16, tag="y_pooled", name="y_pooled", bufs=1, align_bytes=64)
            elif (g, h) not in y_grouped:
                t = work.tile([P, HALF_A, PACK], BF16, tag="y_grouped", name="y_grouped", align_bytes=64)
                y_grouped[g, h] = t
            else:
                t = y_grouped[g, h]
            src = y_planes[g, h][:, :, a0:a1]
            if engine is nc.gpsimd:
                nc.gpsimd.tensor_scalar(
                    out=t[:], in0=src.rearrange("p j a -> p a j"),
                    scalar1=1.0, scalar2=0.0, op0=MULT, op1=ADD,
                )
                y_pooled[g, h, a0] = t
            else:
                interleave(engine, t[:, a0:a1, :], src)

        def quantise_y(g, h, a0, a1, pooled=False):
            cols = slice(HALF_A * h + a0, HALF_A * h + a1)
            if pooled:
                src = y_pooled[g, h, a0][:]
            else:
                src = y_grouped[g, h][:, a0:a1, :]
            nc.vector.quantize_mx(
                out=y_codes[g][:, cols].bitcast(FP8X4),
                scales=y_scales[g][:, cols],
                in_=src.rearrange("p a j -> p (a j)"),
            )

        cov_banks = {}

        def multiply_cov(m, h, g):
            if g == 0:
                b = 4 + m if h == 0 else m
                cov_banks[m, h] = bank(b, "cov_sum")
            c_cols = slice(P * m, P * (m + 1))
            a_cols = slice(HALF_A * h, HALF_A * (h + 1))
            nc.tensor.matmul_mx(
                out=cov_banks[m, h][:],
                lhsT=z_codes[g][:, c_cols].bitcast(FP8X4),
                lhsT_scale=z_scales[g][:, c_cols],
                rhs=y_codes[g][:, a_cols].bitcast(FP8X4),
                rhs_scale=y_scales[g][:, a_cols],
                start=(g == 0),
                stop=(g == G_S - 1),
            )

        def store_cov(m, h, engine):
            res = keep.tile([P, HALF_A], F32, name=f"res{m}{h}")
            if engine is nc.vector:
                nc.vector.tensor_scalar(
                    out=res[:], in0=cov_banks[m, h][:], scalar1=inv_sb[:, m : m + 1],
                    scalar2=None, op0=MULT,
                )
            else:
                nc.scalar.activation(res[:], cov_banks[m, h][:], COPY, scale=inv_sb[:, m : m + 1])
            nc.sync.dma_start(
                out=out[P * m : P * (m + 1), HALF_A * h : HALF_A * (h + 1)], in_=res[:]
            )

        chunks = [(0, 0), (1, 0), (0, 1), (2, 0), (1, 1), (3, 0), (2, 1), (3, 1)]
        last = G_S - 1

        idle = bank(7, "idle")
        for n in range(3):
            nc.tensor.matmul(idle[:], lhsT=zeros[:, :P], rhs=zeros[:], start=True, stop=True)
        transpose_x(0)
        interleave_r(0, 0, C, nc.scalar)
        interleave_r(2, 0, C, nc.scalar)
        for i in range(N_TILES):
            n, piece = (i - 2) // 2, (i - 2) % 2
            if i > 1:
                interleave_y(*chunks[n], 128 * piece, 128 * (piece + 1), nc.gpsimd)
            centre_x(i, 0)
            centre_x(i, 1)
            if i > 2 and i % 2 == 1 and i < 15:
                quantise_y(*chunks[(i - 3) // 2], 256, HALF_A)
            quantise_x(i, 0)
            quantise_x(i, 1)
            if i == 1:
                nc.vector.tensor_copy(
                    out=weight_sb[:], in_=weight_bf[:].rearrange("p g j -> p (g j)")
                )
                nc.vector.tensor_copy(out=inv_sb[:], in_=inv_bf[:, :, 0])
            if i + 1 < N_TILES:
                transpose_x(i + 1)
            if i == 0:
                interleave_r(1, 0, C, nc.vector)
                quantise_r(0)
                quantise_r(1)
                interleave_r(3, 384, C, nc.scalar)
                interleave_r(3, 0, 384, nc.vector)
                quantise_r(2)
                quantise_r(3)
            if i + 1 < N_TILES:
                multiply_t(i, 2 + i % 2, 0, C)
            else:
                for m in range(4):
                    multiply_cov(m, 0, 2)
                multiply_t(i, 3, 0, 256)
                multiply_t(i, 1, 256, C)
            if i % PACK == 1 and i > 1:
                interleave_z(i // PACK - 1, 384, C, nc.scalar)
                interleave_z(i // PACK - 1, 0, 384, nc.vector)
            if i % PACK == 2 and i > 2:
                quantise_z(i // PACK - 1, 0, C)
            if i % 2 == 1 and i < 15:
                widen_y(*chunks[(i - 1) // 2])
            elif i % 2 == 0 and i > 0:
                interleave_y(*chunks[(i - 2) // 2], 256, HALF_A, nc.scalar)
            if i == 14:
                widen_y(*chunks[7])
            if i > 0:
                weigh_t(i - 1, 0, C)
            if i + 1 == N_TILES:
                weigh_t(i, 0, 256)
                weigh_t(i, 256, C)
            if i > 1:
                quantise_y(*chunks[n], 128 * piece, 128 * (piece + 1), pooled=True)
            if i in (7, 8, 9, 10, 11, 12, 13, 14):
                multiply_cov((i - 7) % PACK, 0, (i - 7) // PACK)

        quantise_y(2, 1, 256, HALF_A)
        interleave_y(3, 1, 0, 128, nc.gpsimd)
        interleave_y(3, 1, 320, HALF_A, nc.scalar)
        interleave_y(3, 1, 128, 320, nc.vector)
        quantise_y(3, 1, 0, 128, pooled=True)
        for m in (0, 2):
            for g in range(G_S - 1):
                multiply_cov(m, 1, g)
        interleave_z(last, 0, 256, nc.vector)
        quantise_y(3, 1, 128, 256)
        interleave_z(last, 256, C, nc.vector)
        quantise_z(last, 0, 256)
        quantise_z(last, 256, C)
        quantise_y(3, 1, 256, HALF_A)
        for m in range(4):
            multiply_cov(m, 0, last)
            store_cov(m, 0, nc.vector if m % 2 else nc.scalar)
        for m in (3, 1):
            for g in range(G_S - 1):
                multiply_cov(m, 1, g)
        for m in (0, 2, 3, 1):
            multiply_cov(m, 1, last)
            store_cov(m, 1, nc.vector if m in (2, 1) else nc.scalar)
